import numpy as np
CORES = [2,47,145,220,251]
N = 5
def setup_inputs(rng):
    return {"x": rng.standard_normal((N, 128, 8), dtype=np.float32)}
def reference(x):
    s = x.max(axis=0)
    return {"y": np.broadcast_to(s, (N,) + s.shape)}

@@ -1,0 +1,70 @@
+from concourse.bass import RemoteDMATransfer, DstId
+
+W = 8
+SCRATCH = {
+    "sx": ("sbuf", [128, W], "float32"),
+    "land": ("sbuf", [128, 5 * W], "float32"),
+    "res": ("sbuf", [128, W], "float32"),
+}
+SEMAPHORES = ["ldst", "sent", "own", "got", "res"]
+
+LO, HI, ALL = 0x00FF, 0xFF00, 0xFFFF
+
+
+def folder_of(r, topo):
+    base = r - r % 8
+    return [c for c in range(base, base + 8) if c != r and c % 8 in (2, 3, 6, 7) and topo.die(c) == topo.die(r)][0]
+
+
+def rank_program(g, core, T, topo):
+    ranks = list(T.cores)
+    fold = {r: folder_of(r, topo) for r in ranks}
+
+    def ids(dsts):
+        out = []
+        for d in dsts:
+            rid, pid = topo.addr(d, core)
+            out.append(DstId(rid=rid, pnc=pid))
+        return out
+
+    def slot(i):
+        return T.land[:, i * W:(i + 1) * W]
+
+    rank = T.rank_of(core)
+    if rank is not None:
+        direct = [fold[q] for q in ranks if q != core and topo.may_write(core, fold[q])]
+        g.dma_start(T.sx[:], T.x[:]).then_inc(T.sem.ldst, 16)
+        g.wait_ge(T.sem.ldst, 16)
+        g.remote_dma_fused([
+            RemoteDMATransfer(dst_ids=ids([fold[core]]), dma_engine_mask=HI, remote_sem=T.sem.own,
+                              srcs=[T.sx[:]], dsts=[slot(rank)], alu_op=0),
+            RemoteDMATransfer(dst_ids=ids(direct), dma_engine_mask=LO, remote_sem=T.sem.got,
+                              srcs=[T.sx[:]], dsts=[slot(rank)] * len(direct), alu_op=0),
+        ], local_sem=T.sem.sent)
+        g.wait_ge(T.sem.sent, 16)
+        g.wait_ge(T.sem.res, 16)
+        g.dma_start(T.y[:], T.res[:]).then_inc(T.sem.ldst, 16)
+        g.wait_ge(T.sem.ldst, 32)
+        return
+
+    mine = [r for r in ranks if fold[r] == core]
+    if not mine:
+        return
+    r = mine[0]
+    i = T.rank_of(r)
+    relay = [fold[q] for q in ranks if q != r and not topo.may_write(r, fold[q])]
+    sent = 0
+    g.wait_ge(T.sem.own, 8)
+    if relay:
+        g.remote_dma_fused([
+            RemoteDMATransfer(dst_ids=ids(relay), dma_engine_mask=LO, remote_sem=T.sem.got,
+                              srcs=[slot(i)], dsts=[slot(i)] * len(relay), alu_op=0),
+        ], local_sem=T.sem.sent)
+        sent += 8
+    g.wait_ge(T.sem.got, 8 * (len(ranks) - 1))
+    g.remote_dma_fused([
+        RemoteDMATransfer(dst_ids=ids([r]), dma_engine_mask=ALL, remote_sem=T.sem.res,
+                          srcs=[slot(k) for k in range(len(ranks))], dsts=[T.res[:]], alu_op=2),
+    ], local_sem=T.sem.sent)
+    sent += 16
+    g.wait_ge(T.sem.sent, sent)

@@ -2,9 +2,9 @@ from concourse.bass import RemoteDMATransfer, DstId
 
 W = 8
 SCRATCH = {
-    "sx": ("sbuf", [128, W], "float32"),
-    "land": ("sbuf", [128, 5 * W], "float32"),
-    "res": ("sbuf", [128, W], "float32"),
+    "sx": ("dram", [128, W], "float32"),
+    "land": ("dram", [5, 128, W], "float32"),
+    "res": ("dram", [128, W], "float32"),
 }
 SEMAPHORES = ["ldst", "sent", "own", "got", "res"]
 
@@ -28,7 +28,7 @@ def rank_program(g, core, T, topo):
         return out
 
     def slot(i):
-        return T.land[:, i * W:(i + 1) * W]
+        return T.land[i]
 
     rank = T.rank_of(core)
     if rank is not None:

@@ -11,60 +11,68 @@ SEMAPHORES = ["ldst", "sent", "own", "got", "res"]
 LO, HI, ALL = 0x00FF, 0xFF00, 0xFFFF
 
 
-def folder_of(r, topo):
+def port_owner(r, topo, same_die):
     base = r - r % 8
-    return [c for c in range(base, base + 8) if c != r and c % 8 in (2, 3, 6, 7) and topo.die(c) == topo.die(r)][0]
+    return [c for c in range(base, base + 8)
+            if c != r and c % 8 in (2, 3, 6, 7) and (topo.die(c) == topo.die(r)) == same_die][0]
 
 
 def rank_program(g, core, T, topo):
     ranks = list(T.cores)
-    fold = {r: folder_of(r, topo) for r in ranks}
+    n = len(ranks)
+    fold = {r: port_owner(r, topo, True) for r in ranks}
 
-    def ids(dsts):
-        out = []
-        for d in dsts:
+    def relays(r):
+        d = [fold[q] for q in ranks if q != r and not topo.may_write(r, fold[q])]
+        if not d:
+            return {}
+        d.sort(key=lambda f: topo.die(f) == topo.die(r))
+        k = (len(d) + 1) // 2
+        return {port_owner(r, topo, False): d[:k], fold[r]: d[k:]}
+
+    def copy(src, dst, to, mask, sem):
+        ids = []
+        for d in to:
             rid, pid = topo.addr(d, core)
-            out.append(DstId(rid=rid, pnc=pid))
-        return out
-
-    def slot(i):
-        return T.land[i]
+            ids.append(DstId(rid=rid, pnc=pid))
+        return RemoteDMATransfer(dst_ids=ids, dma_engine_mask=mask, remote_sem=sem,
+                                 srcs=[src], dsts=[dst] * len(to), alu_op=0)
 
     rank = T.rank_of(core)
     if rank is not None:
         direct = [fold[q] for q in ranks if q != core and topo.may_write(core, fold[q])]
         g.dma_start(T.sx[:], T.x[:]).then_inc(T.sem.ldst, 16)
         g.wait_ge(T.sem.ldst, 16)
-        g.remote_dma_fused([
-            RemoteDMATransfer(dst_ids=ids([fold[core]]), dma_engine_mask=HI, remote_sem=T.sem.own,
-                              srcs=[T.sx[:]], dsts=[slot(rank)], alu_op=0),
-            RemoteDMATransfer(dst_ids=ids(direct), dma_engine_mask=LO, remote_sem=T.sem.got,
-                              srcs=[T.sx[:]], dsts=[slot(rank)] * len(direct), alu_op=0),
-        ], local_sem=T.sem.sent)
-        g.wait_ge(T.sem.sent, 16)
+        if relays(core):
+            g.remote_dma_fused([copy(T.sx[:], T.land[rank], list(relays(core)), ALL, T.sem.own)], local_sem=T.sem.sent)
+            g.remote_dma_fused([copy(T.sx[:], T.land[rank], direct, LO, T.sem.got)], local_sem=T.sem.sent)
+            g.wait_ge(T.sem.sent, 24)
+        else:
+            g.remote_dma_fused([copy(T.sx[:], T.land[rank], [fold[core]], HI, T.sem.own),
+                                copy(T.sx[:], T.land[rank], direct, LO, T.sem.got)], local_sem=T.sem.sent)
+            g.wait_ge(T.sem.sent, 16)
         g.wait_ge(T.sem.res, 16)
         g.dma_start(T.y[:], T.res[:]).then_inc(T.sem.ldst, 16)
         g.wait_ge(T.sem.ldst, 32)
         return
 
-    mine = [r for r in ranks if fold[r] == core]
-    if not mine:
+    for r in ranks:
+        i = T.rank_of(r)
+        serve = relays(r).get(core, [])
+        if core != fold[r] and not serve:
+            continue
+        sent = 0
+        g.wait_ge(T.sem.own, 16 if relays(r) else 8)
+        if serve:
+            g.remote_dma_fused([copy(T.land[i], T.land[i], serve, LO, T.sem.got)], local_sem=T.sem.sent)
+            sent += 8
+        if core == fold[r]:
+            g.wait_ge(T.sem.got, 8 * (n - 1))
+            rid, pid = topo.addr(r, core)
+            g.remote_dma_fused([
+                RemoteDMATransfer(dst_ids=[DstId(rid=rid, pnc=pid)], dma_engine_mask=ALL, remote_sem=T.sem.res,
+                                  srcs=[T.land[k] for k in range(n)], dsts=[T.res[:]], alu_op=2),
+            ], local_sem=T.sem.sent)
+            sent += 16
+        g.wait_ge(T.sem.sent, sent)
         return
-    r = mine[0]
-    i = T.rank_of(r)
-    relay = [fold[q] for q in ranks if q != r and not topo.may_write(r, fold[q])]
-    sent = 0
-    g.wait_ge(T.sem.own, 8)
-    if relay:
-        g.remote_dma_fused([
-            RemoteDMATransfer(dst_ids=ids(relay), dma_engine_mask=LO, remote_sem=T.sem.got,
-                              srcs=[slot(i)], dsts=[slot(i)] * len(relay), alu_op=0),
-        ], local_sem=T.sem.sent)
-        sent += 8
-    g.wait_ge(T.sem.got, 8 * (len(ranks) - 1))
-    g.remote_dma_fused([
-        RemoteDMATransfer(dst_ids=ids([r]), dma_engine_mask=ALL, remote_sem=T.sem.res,
-                          srcs=[slot(k) for k in range(len(ranks))], dsts=[T.res[:]], alu_op=2),
-    ], local_sem=T.sem.sent)
-    sent += 16
-    g.wait_ge(T.sem.sent, sent)

from concourse.bass import RemoteDMATransfer, DstId

W = 8
SCRATCH = {
    "sx": ("dram", [128, W], "float32"),
    "land": ("dram", [5, 128, W], "float32"),
    "res": ("dram", [128, W], "float32"),
}
SEMAPHORES = ["ldst", "sent", "own", "got", "res"]

LO, HI, ALL = 0x00FF, 0xFF00, 0xFFFF


def port_owner(r, topo, same_die):
    base = r - r % 8
    return [c for c in range(base, base + 8)
            if c != r and c % 8 in (2, 3, 6, 7) and (topo.die(c) == topo.die(r)) == same_die][0]


def rank_program(g, core, T, topo):
    ranks = list(T.cores)
    n = len(ranks)
    fold = {r: port_owner(r, topo, True) for r in ranks}

    def relays(r):
        d = [fold[q] for q in ranks if q != r and not topo.may_write(r, fold[q])]
        if not d:
            return {}
        d.sort(key=lambda f: topo.die(f) == topo.die(r))
        k = (len(d) + 1) // 2
        return {port_owner(r, topo, False): d[:k], fold[r]: d[k:]}

    def copy(src, dst, to, mask, sem):
        ids = []
        for d in to:
            rid, pid = topo.addr(d, core)
            ids.append(DstId(rid=rid, pnc=pid))
        return RemoteDMATransfer(dst_ids=ids, dma_engine_mask=mask, remote_sem=sem,
                                 srcs=[src], dsts=[dst] * len(to), alu_op=0)

    rank = T.rank_of(core)
    if rank is not None:
        direct = [fold[q] for q in ranks if q != core and topo.may_write(core, fold[q])]
        g.dma_start(T.sx[:], T.x[:]).then_inc(T.sem.ldst, 16)
        g.wait_ge(T.sem.ldst, 16)
        if relays(core):
            g.remote_dma_fused([copy(T.sx[:], T.land[rank], list(relays(core)), ALL, T.sem.own)], local_sem=T.sem.sent)
            g.remote_dma_fused([copy(T.sx[:], T.land[rank], direct, LO, T.sem.got)], local_sem=T.sem.sent)
            g.wait_ge(T.sem.sent, 24)
        else:
            g.remote_dma_fused([copy(T.sx[:], T.land[rank], [fold[core]], HI, T.sem.own),
                                copy(T.sx[:], T.land[rank], direct, LO, T.sem.got)], local_sem=T.sem.sent)
            g.wait_ge(T.sem.sent, 16)
        g.wait_ge(T.sem.res, 16)
        g.dma_start(T.y[:], T.res[:]).then_inc(T.sem.ldst, 16)
        g.wait_ge(T.sem.ldst, 32)
        return

    for r in ranks:
        i = T.rank_of(r)
        serve = relays(r).get(core, [])
        if core != fold[r] and not serve:
            continue
        sent = 0
        g.wait_ge(T.sem.own, 16 if relays(r) else 8)
        if serve:
            g.remote_dma_fused([copy(T.land[i], T.land[i], serve, LO, T.sem.got)], local_sem=T.sem.sent)
            sent += 8
        if core == fold[r]:
            g.wait_ge(T.sem.got, 8 * (n - 1))
            rid, pid = topo.addr(r, core)
            g.remote_dma_fused([
                RemoteDMATransfer(dst_ids=[DstId(rid=rid, pnc=pid)], dma_engine_mask=ALL, remote_sem=T.sem.res,
                                  srcs=[T.land[k] for k in range(n)], dsts=[T.res[:]], alu_op=2),
            ], local_sem=T.sem.sent)
            sent += 16
        g.wait_ge(T.sem.sent, sent)
        return
